import numpy as np
import ml_dtypes


def mxq(x, axis, fmt="e4m3"):
    dtype, down = {"e4m3": (ml_dtypes.float8_e4m3fn, 7), "e5m2": (ml_dtypes.float8_e5m2, 14)}[fmt]
    v = np.moveaxis(np.asarray(x, np.float32).astype(ml_dtypes.bfloat16).astype(np.float64), axis, -1)
    blocks = v.reshape(v.shape[:-1] + (-1, 32))
    amax = np.abs(blocks).max(-1, keepdims=True)
    byte = np.maximum(np.where(amax > 0, np.frexp(amax)[1] - 1 + 127, 0) - down, 1)
    scale = np.exp2(byte - 127.0)
    codes = (blocks / scale).astype(np.float32).astype(dtype).astype(np.float64)
    return np.moveaxis((codes * scale).reshape(v.shape), -1, axis)


WIDE = False


def mx_kscale(k):
    if not WIDE:
        return np.ones(k)
    levels = np.array([10, -10, 5, -5, 0])
    if k % 512:
        return np.exp2(np.random.permutation(np.resize(levels, k // 32))).repeat(32)
    a = np.empty((k // 512, 16))
    for p in range(k // 512):
        a[p, :8] = np.random.permutation(np.resize(levels, 8))
        for g in range(8):
            far = levels[np.abs(levels - a[p, g]) >= 10]
            a[p, g + 8] = far[np.random.randint(len(far))]
    return np.exp2(a.ravel()).repeat(32)


def f64(x):
    return np.asarray(x).astype(np.float64)


def striped(idx):
    return np.tile(idx.reshape(-1, 16).T, (8, 1)).astype(np.uint16)


def unstriped(offs):
    return offs[:16].T.reshape(-1).astype(np.int64)


K, T, S, V, N = 512, 2048, 1024, 512, 128


def setup_inputs():
    n = np.random.standard_normal
    s = mx_kscale(K)[:, None]
    return {
        "xT": (n((K, T)) * s).astype(np.float32),
        "w1": (n((K, N)) / np.sqrt(K) / s).astype(np.float32),
        "offs": striped(np.random.permutation(T)[:S]),
        "win": striped(np.random.permutation(S)[:V]),
        "lose": striped(np.random.permutation(S)[:V]),
    }


def reference(xT, w1, offs, win, lose):
    xq = mxq(f64(xT)[:, unstriped(offs)], 0, "e4m3")
    y = mxq(f64(w1), 0, "e4m3").T @ xq
    return np.tanh(y[:, unstriped(win)] - y[:, unstriped(lose)])

@@ -1,0 +1,138 @@
+from contextlib import ExitStack
+
+import concourse.mybir as mybir
+
+K, T, S, V, N = 512, 2048, 1024, 512, 128
+FLOPS = 2 * K * S * N
+
+F32 = mybir.dt.float32
+BF16 = mybir.dt.bfloat16
+U32 = mybir.dt.uint32
+U16 = mybir.dt.uint16
+U8 = mybir.dt.uint8
+FP8X4 = mybir.dt.float8_e4m3fn_x4
+
+P = 128
+PIECE = 256
+CHUNKS = ((1024, 512, 512), (512, 512, 512, 256, 256))
+QUANT = (512, 256, 128, 128)
+PAIRS = (256, 128, 128)
+
+
+def tile_picked_ranknet_tanh_e_kernel(tc, xT, w1, offs, win, lose, out):
+    nc = tc.nc
+    with ExitStack() as ctx:
+        keep = ctx.enter_context(tc.tile_pool(name="keep", bufs=1))
+        psum = ctx.enter_context(tc.psum_pool(name="psum", bufs=1))
+
+        offs_t = keep.tile([P, S // 16], U16, name="offs_t")
+        win_t = keep.tile([P, V // 16], U16, name="win_t")
+        lose_t = keep.tile([P, V // 16], U16, name="lose_t")
+        w_raw = keep.tile([P, 4, N], F32, name="w_raw")
+        x_rows = xT.rearrange("(p j) t -> p j t", j=4)
+
+        raw = {}
+
+        def load(u, c):
+            c0 = sum(CHUNKS[u][:c])
+            width = CHUNKS[u][c]
+            raw[u, c] = keep.tile([P, 2, width], F32, name="raw_%d_%d" % (u, c))
+            nc.sync.dma_start(out=raw[u, c][:], in_=x_rows[:, 2 * u : 2 * u + 2, c0 : c0 + width])
+
+        load(0, 0)
+        load(0, 1)
+        load(0, 2)
+        nc.sync.dma_start(offs_t[:], offs)
+        for c in range(len(CHUNKS[1])):
+            load(1, c)
+        nc.sync.dma_start(out=w_raw[:], in_=w1.rearrange("(p j) n -> p j n", j=4))
+        nc.sync.dma_start(lose_t[:], lose)
+        nc.sync.dma_start(win_t[:], win)
+
+        pairs = [keep.tile([P, 2 * T], BF16, name="pairs_%d" % u, align_bytes=64) for u in range(2)]
+
+        def cast(engine, u, c, a, b):
+            c0 = sum(CHUNKS[u][:c])
+            dst = pairs[u][:, 2 * (c0 + a) : 2 * (c0 + b)].rearrange("p (t e) -> p t e", e=2)
+            src = raw[u, c][:, :, a:b].rearrange("p e t -> p t e")
+            if engine == "vector":
+                nc.vector.tensor_copy(out=dst, in_=src)
+            else:
+                nc.scalar.copy(out=dst, in_=src)
+
+        halves = keep.tile([P, 2, S], U32, name="halves", align_bytes=64)
+
+        cast("vector", 0, 0, 0, 1024)
+        cast("vector", 0, 1, 0, 512)
+        cast("vector", 0, 2, 0, 352)
+        cast("scalar", 0, 2, 352, 512)
+        nc.vector.tensor_copy(out=halves[:, 0, :], in_=pairs[0][:].bitcast(U32).indirect(offs_t[:]))
+
+        w_bf = keep.tile([P, N * 4], BF16, name="w_bf", align_bytes=64)
+        w_codes = keep.tile([P, N], U32, name="w_codes", align_bytes=64)
+        w_scales = keep.tile([P, N], U8, name="w_scales", align_bytes=64)
+        cast("scalar", 1, 0, 0, 512)
+        cast("scalar", 1, 1, 0, 512)
+        cast("vector", 1, 2, 0, 512)
+        cast("vector", 1, 3, 0, 256)
+        cast("vector", 1, 4, 0, 192)
+        cast("scalar", 1, 4, 192, 256)
+
+        nc.scalar.copy(out=w_bf[:].rearrange("p (n j) -> p n j", j=4), in_=w_raw[:].rearrange("p j n -> p n j"))
+        woven = [
+            keep.tile([P, 4 * width], BF16, name="woven_%d" % i, align_bytes=64) for i, width in enumerate((512, 256, 256))
+        ]
+        home = {0: (0, 0), 256: (0, 256), 512: (1, 0), 768: (2, 0), 896: (2, 128)}
+        for i in range(S // PIECE):
+            s0 = i * PIECE
+            nc.vector.tensor_copy(
+                out=halves[:, 1, s0 : s0 + PIECE],
+                in_=pairs[1][:].bitcast(U32).indirect(offs_t[:, s0 // 16 : (s0 + PIECE) // 16]),
+            )
+            t, a = home[s0]
+            nc.scalar.copy(
+                out=woven[t][:, 4 * a : 4 * (a + PIECE)].bitcast(U32).rearrange("p (s u) -> p s u", u=2),
+                in_=halves[:, :, s0 : s0 + PIECE].rearrange("p u s -> p s u"),
+            )
+
+        nc.vector.quantize_mx(out=w_codes[:].bitcast(FP8X4), scales=w_scales[:], in_=w_bf[:])
+        y = keep.tile([P, S], F32, name="y")
+        s0 = 0
+        for i, width in enumerate(QUANT):
+            codes = keep.tile([P, width], U32, name="codes_%d" % i, align_bytes=64)
+            scales = keep.tile([P, width], U8, name="scales_%d" % i, align_bytes=64)
+            t, a = home[s0]
+            nc.vector.quantize_mx(
+                out=codes[:].bitcast(FP8X4), scales=scales[:], in_=woven[t][:, 4 * a : 4 * (a + width)]
+            )
+            acc = psum.tile([P, width], F32, name="acc_%d" % i)
+            nc.tensor.matmul_mx(
+                out=acc[:],
+                lhsT=w_codes[:].bitcast(FP8X4),
+                lhsT_scale=w_scales[:],
+                rhs=codes[:].bitcast(FP8X4),
+                rhs_scale=scales[:],
+                start=True,
+                stop=True,
+            )
+            nc.scalar.copy(out=y[:, s0 : s0 + width], in_=acc[:])
+            s0 += width
+
+        y_lose = keep.tile([P, V], F32, name="y_lose")
+        for h in range(2):
+            nc.vector.tensor_copy(
+                out=y_lose[:, 256 * h : 256 * (h + 1)], in_=y[:].indirect(lose_t[:, 16 * h : 16 * (h + 1)])
+            )
+        v0 = 0
+        for i, width in enumerate(PAIRS):
+            diff = keep.tile([P, width], F32, name="diff_%d" % i)
+            nc.vector.tensor_tensor(
+                out=diff[:],
+                in0=y[:].indirect(win_t[:, v0 // 16 : (v0 + width) // 16]),
+                in1=y_lose[:, v0 : v0 + width],
+                op=mybir.AluOpType.subtract,
+            )
+            res = keep.tile([P, width], F32, name="res_%d" % i)
+            nc.scalar.activation(out=res[:], in_=diff[:], func=mybir.ActivationFunctionType.Tanh)
+            (nc.scalar if i == len(PAIRS) - 1 else nc.sync).dma_start(out=out[:, v0 : v0 + width], in_=res[:])
+            v0 += width

@@ -14,9 +14,10 @@ FP8X4 = mybir.dt.float8_e4m3fn_x4
 
 P = 128
 PIECE = 256
-CHUNKS = ((1024, 512, 512), (512, 512, 512, 256, 256))
-QUANT = (512, 256, 128, 128)
-PAIRS = (256, 128, 128)
+FIRST_CHUNKS = (1024, 1024)
+LAST_CHUNKS = (512, 256, 256)
+QUANT = (256, 256, 256, 128, 128)
+PAIRS = (256, 192, 64)
 
 
 def tile_picked_ranknet_tanh_e_kernel(tc, xT, w1, offs, win, lose, out):
@@ -31,69 +32,63 @@ def tile_picked_ranknet_tanh_e_kernel(tc, xT, w1, offs, win, lose, out):
         w_raw = keep.tile([P, 4, N], F32, name="w_raw")
         x_rows = xT.rearrange("(p j) t -> p j t", j=4)
 
-        raw = {}
-
-        def load(u, c):
-            c0 = sum(CHUNKS[u][:c])
-            width = CHUNKS[u][c]
-            raw[u, c] = keep.tile([P, 2, width], F32, name="raw_%d_%d" % (u, c))
-            nc.sync.dma_start(out=raw[u, c][:], in_=x_rows[:, 2 * u : 2 * u + 2, c0 : c0 + width])
-
-        load(0, 0)
-        load(0, 1)
-        load(0, 2)
+        first = [keep.tile([P, 2, width], F32, name="first_%d" % c) for c, width in enumerate(FIRST_CHUNKS)]
+        second_a = keep.tile([P, 2, T // 2], F32, name="second_a")
+        second = keep.tile([P, 2, T // 2], F32, name="second")
+        for c, width in enumerate(FIRST_CHUNKS):
+            nc.sync.dma_start(out=first[c][:], in_=x_rows[:, 0:2, c * width : (c + 1) * width])
         nc.sync.dma_start(offs_t[:], offs)
-        for c in range(len(CHUNKS[1])):
-            load(1, c)
+        nc.sync.dma_start(out=second_a[:], in_=x_rows[:, 2:4, : T // 2])
+        nc.sync.dma_start(out=second[:, 0, :], in_=x_rows[:, 2, T // 2 :])
+        c0 = 0
+        for width in LAST_CHUNKS:
+            nc.sync.dma_start(out=second[:, 1, c0 : c0 + width], in_=x_rows[:, 3, T // 2 + c0 : T // 2 + c0 + width])
+            c0 += width
         nc.sync.dma_start(out=w_raw[:], in_=w1.rearrange("(p j) n -> p j n", j=4))
         nc.sync.dma_start(lose_t[:], lose)
         nc.sync.dma_start(win_t[:], win)
 
         pairs = [keep.tile([P, 2 * T], BF16, name="pairs_%d" % u, align_bytes=64) for u in range(2)]
 
-        def cast(engine, u, c, a, b):
-            c0 = sum(CHUNKS[u][:c])
-            dst = pairs[u][:, 2 * (c0 + a) : 2 * (c0 + b)].rearrange("p (t e) -> p t e", e=2)
-            src = raw[u, c][:, :, a:b].rearrange("p e t -> p t e")
-            if engine == "vector":
-                nc.vector.tensor_copy(out=dst, in_=src)
-            else:
-                nc.scalar.copy(out=dst, in_=src)
+        def cast(u, src, c0, width, share=11):
+            cut = width * share // 16
+            for copy, a, b in ((nc.vector.tensor_copy, 0, cut), (nc.scalar.copy, cut, width)):
+                copy(
+                    out=pairs[u][:, 2 * (c0 + a) : 2 * (c0 + b)].rearrange("p (t e) -> p t e", e=2),
+                    in_=src[:, :, a:b].rearrange("p e t -> p t e"),
+                )
 
         halves = keep.tile([P, 2, S], U32, name="halves", align_bytes=64)
 
-        cast("vector", 0, 0, 0, 1024)
-        cast("vector", 0, 1, 0, 512)
-        cast("vector", 0, 2, 0, 352)
-        cast("scalar", 0, 2, 352, 512)
+        for c, width in enumerate(FIRST_CHUNKS):
+            cast(0, first[c][:], c * width, width)
         nc.vector.tensor_copy(out=halves[:, 0, :], in_=pairs[0][:].bitcast(U32).indirect(offs_t[:]))
 
         w_bf = keep.tile([P, N * 4], BF16, name="w_bf", align_bytes=64)
         w_codes = keep.tile([P, N], U32, name="w_codes", align_bytes=64)
         w_scales = keep.tile([P, N], U8, name="w_scales", align_bytes=64)
-        cast("scalar", 1, 0, 0, 512)
-        cast("scalar", 1, 1, 0, 512)
-        cast("vector", 1, 2, 0, 512)
-        cast("vector", 1, 3, 0, 256)
-        cast("vector", 1, 4, 0, 192)
-        cast("scalar", 1, 4, 192, 256)
+        cast(1, second_a[:], 0, T // 2, share=6)
+        c0 = 0
+        for width in LAST_CHUNKS:
+            cast(1, second[:, :, c0 : c0 + width], T // 2 + c0, width)
+            c0 += width
 
-        nc.scalar.copy(out=w_bf[:].rearrange("p (n j) -> p n j", j=4), in_=w_raw[:].rearrange("p j n -> p n j"))
-        woven = [
-            keep.tile([P, 4 * width], BF16, name="woven_%d" % i, align_bytes=64) for i, width in enumerate((512, 256, 256))
-        ]
-        home = {0: (0, 0), 256: (0, 256), 512: (1, 0), 768: (2, 0), 896: (2, 128)}
+        nc.scalar.copy(
+            out=w_bf[:].rearrange("p (c i j) -> p c j i", i=4, j=4), in_=w_raw[:].rearrange("p j (c i) -> p c j i", i=4)
+        )
+        woven = []
         for i in range(S // PIECE):
             s0 = i * PIECE
             nc.vector.tensor_copy(
                 out=halves[:, 1, s0 : s0 + PIECE],
                 in_=pairs[1][:].bitcast(U32).indirect(offs_t[:, s0 // 16 : (s0 + PIECE) // 16]),
             )
-            t, a = home[s0]
+            g = keep.tile([P, 4 * PIECE], BF16, name="woven_%d" % i, align_bytes=64)
             nc.scalar.copy(
-                out=woven[t][:, 4 * a : 4 * (a + PIECE)].bitcast(U32).rearrange("p (s u) -> p s u", u=2),
+                out=g[:].bitcast(U32).rearrange("p (s u) -> p s u", u=2),
                 in_=halves[:, :, s0 : s0 + PIECE].rearrange("p u s -> p s u"),
             )
+            woven.append(g)
 
         nc.vector.quantize_mx(out=w_codes[:].bitcast(FP8X4), scales=w_scales[:], in_=w_bf[:])
         y = keep.tile([P, S], F32, name="y")
@@ -101,9 +96,9 @@ def tile_picked_ranknet_tanh_e_kernel(tc, xT, w1, offs, win, lose, out):
         for i, width in enumerate(QUANT):
             codes = keep.tile([P, width], U32, name="codes_%d" % i, align_bytes=64)
             scales = keep.tile([P, width], U8, name="scales_%d" % i, align_bytes=64)
-            t, a = home[s0]
+            a = s0 % PIECE
             nc.vector.quantize_mx(
-                out=codes[:].bitcast(FP8X4), scales=scales[:], in_=woven[t][:, 4 * a : 4 * (a + width)]
+                out=codes[:].bitcast(FP8X4), scales=scales[:], in_=woven[s0 // PIECE][:, 4 * a : 4 * (a + width)]
             )
             acc = psum.tile([P, width], F32, name="acc_%d" % i)
             nc.tensor.matmul_mx(

@@ -54,8 +54,8 @@ def tile_picked_ranknet_tanh_e_kernel(tc, xT, w1, offs, win, lose, out):
             cut = width * share // 16
             for copy, a, b in ((nc.vector.tensor_copy, 0, cut), (nc.scalar.copy, cut, width)):
                 copy(
-                    out=pairs[u][:, 2 * (c0 + a) : 2 * (c0 + b)].rearrange("p (t e) -> p t e", e=2),
-                    in_=src[:, :, a:b].rearrange("p e t -> p t e"),
+                    out=pairs[u][:, 2 * (c0 + a) : 2 * (c0 + b)].rearrange("p (c i e) -> p c e i", i=4, e=2),
+                    in_=src[:, :, a:b].rearrange("p e (c i) -> p c e i", i=4),
                 )
 
         halves = keep.tile([P, 2, S], U32, name="halves", align_bytes=64)
@@ -85,8 +85,8 @@ def tile_picked_ranknet_tanh_e_kernel(tc, xT, w1, offs, win, lose, out):
             )
             g = keep.tile([P, 4 * PIECE], BF16, name="woven_%d" % i, align_bytes=64)
             nc.scalar.copy(
-                out=g[:].bitcast(U32).rearrange("p (s u) -> p s u", u=2),
-                in_=halves[:, :, s0 : s0 + PIECE].rearrange("p u s -> p s u"),
+                out=g[:].bitcast(U32).rearrange("p (c i u) -> p c u i", i=4, u=2),
+                in_=halves[:, :, s0 : s0 + PIECE].rearrange("p u (c i) -> p c u i", i=4),
             )
             woven.append(g)
 

@@ -14,8 +14,7 @@ FP8X4 = mybir.dt.float8_e4m3fn_x4
 
 P = 128
 PIECE = 256
-FIRST_CHUNKS = (1024, 1024)
-LAST_CHUNKS = (512, 256, 256)
+CHUNKS = ((1024, 512, 512), (512, 512, 512, 256, 256))
 QUANT = (256, 256, 256, 128, 128)
 PAIRS = (256, 192, 64)
 
@@ -32,50 +31,54 @@ def tile_picked_ranknet_tanh_e_kernel(tc, xT, w1, offs, win, lose, out):
         w_raw = keep.tile([P, 4, N], F32, name="w_raw")
         x_rows = xT.rearrange("(p j) t -> p j t", j=4)
 
-        first = [keep.tile([P, 2, width], F32, name="first_%d" % c) for c, width in enumerate(FIRST_CHUNKS)]
-        second_a = keep.tile([P, 2, T // 2], F32, name="second_a")
-        second = keep.tile([P, 2, T // 2], F32, name="second")
-        for c, width in enumerate(FIRST_CHUNKS):
-            nc.sync.dma_start(out=first[c][:], in_=x_rows[:, 0:2, c * width : (c + 1) * width])
+        raw = {}
+
+        def load(u, c):
+            c0 = sum(CHUNKS[u][:c])
+            width = CHUNKS[u][c]
+            raw[u, c] = keep.tile([P, 2, width], F32, name="raw_%d_%d" % (u, c))
+            nc.sync.dma_start(out=raw[u, c][:], in_=x_rows[:, 2 * u : 2 * u + 2, c0 : c0 + width])
+
+        load(0, 0)
+        load(0, 1)
+        load(0, 2)
         nc.sync.dma_start(offs_t[:], offs)
-        nc.sync.dma_start(out=second_a[:], in_=x_rows[:, 2:4, : T // 2])
-        nc.sync.dma_start(out=second[:, 0, :], in_=x_rows[:, 2, T // 2 :])
-        c0 = 0
-        for width in LAST_CHUNKS:
-            nc.sync.dma_start(out=second[:, 1, c0 : c0 + width], in_=x_rows[:, 3, T // 2 + c0 : T // 2 + c0 + width])
-            c0 += width
+        for c in range(len(CHUNKS[1])):
+            load(1, c)
         nc.sync.dma_start(out=w_raw[:], in_=w1.rearrange("(p j) n -> p j n", j=4))
         nc.sync.dma_start(lose_t[:], lose)
         nc.sync.dma_start(win_t[:], win)
 
         pairs = [keep.tile([P, 2 * T], BF16, name="pairs_%d" % u, align_bytes=64) for u in range(2)]
 
-        def cast(u, src, c0, width, share=11):
-            cut = width * share // 16
-            for copy, a, b in ((nc.vector.tensor_copy, 0, cut), (nc.scalar.copy, cut, width)):
-                copy(
-                    out=pairs[u][:, 2 * (c0 + a) : 2 * (c0 + b)].rearrange("p (c i e) -> p c e i", i=4, e=2),
-                    in_=src[:, :, a:b].rearrange("p e (c i) -> p c e i", i=4),
-                )
+        def cast(engine, u, c, a, b):
+            c0 = sum(CHUNKS[u][:c])
+            dst = pairs[u][:, 2 * (c0 + a) : 2 * (c0 + b)].rearrange("p (t e) -> p t e", e=2)
+            src = raw[u, c][:, :, a:b].rearrange("p e t -> p t e")
+            if engine == "vector":
+                nc.vector.tensor_copy(out=dst, in_=src)
+            else:
+                nc.scalar.copy(out=dst, in_=src)
 
         halves = keep.tile([P, 2, S], U32, name="halves", align_bytes=64)
 
-        for c, width in enumerate(FIRST_CHUNKS):
-            cast(0, first[c][:], c * width, width)
+        cast("vector", 0, 0, 0, 1024)
+        cast("vector", 0, 1, 0, 512)
+        cast("vector", 0, 2, 0, 352)
+        cast("scalar", 0, 2, 352, 512)
         nc.vector.tensor_copy(out=halves[:, 0, :], in_=pairs[0][:].bitcast(U32).indirect(offs_t[:]))
 
         w_bf = keep.tile([P, N * 4], BF16, name="w_bf", align_bytes=64)
         w_codes = keep.tile([P, N], U32, name="w_codes", align_bytes=64)
         w_scales = keep.tile([P, N], U8, name="w_scales", align_bytes=64)
-        cast(1, second_a[:], 0, T // 2, share=6)
-        c0 = 0
-        for width in LAST_CHUNKS:
-            cast(1, second[:, :, c0 : c0 + width], T // 2 + c0, width)
-            c0 += width
+        cast("scalar", 1, 0, 0, 512)
+        cast("scalar", 1, 1, 0, 512)
+        cast("vector", 1, 2, 0, 512)
+        cast("vector", 1, 3, 0, 256)
+        cast("vector", 1, 4, 0, 192)
+        cast("scalar", 1, 4, 192, 256)
 
-        nc.scalar.copy(
-            out=w_bf[:].rearrange("p (c i j) -> p c j i", i=4, j=4), in_=w_raw[:].rearrange("p j (c i) -> p c j i", i=4)
-        )
+        nc.scalar.copy(out=w_bf[:].rearrange("p (n j) -> p n j", j=4), in_=w_raw[:].rearrange("p j n -> p n j"))
         woven = []
         for i in range(S // PIECE):
             s0 = i * PIECE
@@ -85,14 +88,15 @@ def tile_picked_ranknet_tanh_e_kernel(tc, xT, w1, offs, win, lose, out):
             )
             g = keep.tile([P, 4 * PIECE], BF16, name="woven_%d" % i, align_bytes=64)
             nc.scalar.copy(
-                out=g[:].bitcast(U32).rearrange("p (c i u) -> p c u i", i=4, u=2),
-                in_=halves[:, :, s0 : s0 + PIECE].rearrange("p u (c i) -> p c u i", i=4),
+                out=g[:].bitcast(U32).rearrange("p (s u) -> p s u", u=2),
+                in_=halves[:, :, s0 : s0 + PIECE].rearrange("p u s -> p s u"),
             )
             woven.append(g)
 
         nc.vector.quantize_mx(out=w_codes[:].bitcast(FP8X4), scales=w_scales[:], in_=w_bf[:])
         y = keep.tile([P, S], F32, name="y")
         s0 = 0
+        banks = []
         for i, width in enumerate(QUANT):
             codes = keep.tile([P, width], U32, name="codes_%d" % i, align_bytes=64)
             scales = keep.tile([P, width], U8, name="scales_%d" % i, align_bytes=64)
@@ -110,8 +114,10 @@ def tile_picked_ranknet_tanh_e_kernel(tc, xT, w1, offs, win, lose, out):
                 start=True,
                 stop=True,
             )
-            nc.scalar.copy(out=y[:, s0 : s0 + width], in_=acc[:])
+            banks.append((s0, width, acc))
             s0 += width
+        for i, (s0, width, acc) in enumerate(banks):
+            (nc.vector.tensor_copy if i == 2 else nc.scalar.copy)(out=y[:, s0 : s0 + width], in_=acc[:])
 
         y_lose = keep.tile([P, V], F32, name="y_lose")
         for h in range(2):

@@ -14,7 +14,6 @@ FP8X4 = mybir.dt.float8_e4m3fn_x4
 
 P = 128
 PIECE = 256
-CHUNKS = ((1024, 512, 512), (512, 512, 512, 256, 256))
 QUANT = (256, 256, 256, 128, 128)
 PAIRS = (256, 192, 64)
 
@@ -31,67 +30,43 @@ def tile_picked_ranknet_tanh_e_kernel(tc, xT, w1, offs, win, lose, out):
         w_raw = keep.tile([P, 4, N], F32, name="w_raw")
         x_rows = xT.rearrange("(p j) t -> p j t", j=4)
 
-        raw = {}
-
-        def load(u, c):
-            c0 = sum(CHUNKS[u][:c])
-            width = CHUNKS[u][c]
-            raw[u, c] = keep.tile([P, 2, width], F32, name="raw_%d_%d" % (u, c))
-            nc.sync.dma_start(out=raw[u, c][:], in_=x_rows[:, 2 * u : 2 * u + 2, c0 : c0 + width])
-
-        load(0, 0)
-        load(0, 1)
-        load(0, 2)
+        raw = [keep.tile([P, T], F32, name="raw_%d" % j) for j in range(4)]
+        nc.sync.dma_start(out=raw[0][:], in_=x_rows[:, 0, :])
         nc.sync.dma_start(offs_t[:], offs)
-        for c in range(len(CHUNKS[1])):
-            load(1, c)
+        for j in range(1, 4):
+            nc.sync.dma_start(out=raw[j][:], in_=x_rows[:, j, :])
         nc.sync.dma_start(out=w_raw[:], in_=w1.rearrange("(p j) n -> p j n", j=4))
         nc.sync.dma_start(lose_t[:], lose)
         nc.sync.dma_start(win_t[:], win)
 
-        pairs = [keep.tile([P, 2 * T], BF16, name="pairs_%d" % u, align_bytes=64) for u in range(2)]
+        halves = keep.tile([P, 2, 2 * S], BF16, name="halves", align_bytes=64)
 
-        def cast(engine, u, c, a, b):
-            c0 = sum(CHUNKS[u][:c])
-            dst = pairs[u][:, 2 * (c0 + a) : 2 * (c0 + b)].rearrange("p (t e) -> p t e", e=2)
-            src = raw[u, c][:, :, a:b].rearrange("p e t -> p t e")
-            if engine == "vector":
-                nc.vector.tensor_copy(out=dst, in_=src)
-            else:
-                nc.scalar.copy(out=dst, in_=src)
+        def gather(j, s0, s1):
+            dst = halves[:, j // 2, 2 * s0 : 2 * s1].rearrange("p (s e) -> p s e", e=2)[:, :, j % 2]
+            nc.vector.tensor_copy(out=dst, in_=raw[j][:].indirect(offs_t[:, s0 // 16 : s1 // 16]))
 
-        halves = keep.tile([P, 2, S], U32, name="halves", align_bytes=64)
-
-        cast("vector", 0, 0, 0, 1024)
-        cast("vector", 0, 1, 0, 512)
-        cast("vector", 0, 2, 0, 352)
-        cast("scalar", 0, 2, 352, 512)
-        nc.vector.tensor_copy(out=halves[:, 0, :], in_=pairs[0][:].bitcast(U32).indirect(offs_t[:]))
+        for j in range(3):
+            gather(j, 0, S)
 
         w_bf = keep.tile([P, N * 4], BF16, name="w_bf", align_bytes=64)
         w_codes = keep.tile([P, N], U32, name="w_codes", align_bytes=64)
         w_scales = keep.tile([P, N], U8, name="w_scales", align_bytes=64)
-        cast("scalar", 1, 0, 0, 512)
-        cast("scalar", 1, 1, 0, 512)
-        cast("vector", 1, 2, 0, 512)
-        cast("vector", 1, 3, 0, 256)
-        cast("vector", 1, 4, 0, 192)
-        cast("scalar", 1, 4, 192, 256)
+        words = halves[:].bitcast(U32)
 
-        nc.scalar.copy(out=w_bf[:].rearrange("p (n j) -> p n j", j=4), in_=w_raw[:].rearrange("p j n -> p n j"))
         woven = []
         for i in range(S // PIECE):
             s0 = i * PIECE
-            nc.vector.tensor_copy(
-                out=halves[:, 1, s0 : s0 + PIECE],
-                in_=pairs[1][:].bitcast(U32).indirect(offs_t[:, s0 // 16 : (s0 + PIECE) // 16]),
-            )
+            gather(3, s0, s0 + PIECE)
             g = keep.tile([P, 4 * PIECE], BF16, name="woven_%d" % i, align_bytes=64)
             nc.scalar.copy(
                 out=g[:].bitcast(U32).rearrange("p (s u) -> p s u", u=2),
-                in_=halves[:, :, s0 : s0 + PIECE].rearrange("p u s -> p s u"),
+                in_=words[:, :, s0 : s0 + PIECE].rearrange("p u s -> p s u"),
             )
             woven.append(g)
+            if i == 0:
+                nc.scalar.copy(
+                    out=w_bf[:].rearrange("p (n j) -> p n j", j=4), in_=w_raw[:].rearrange("p j n -> p n j")
+                )
 
         nc.vector.quantize_mx(out=w_codes[:].bitcast(FP8X4), scales=w_scales[:], in_=w_bf[:])
         y = keep.tile([P, S], F32, name="y")

@@ -14,8 +14,11 @@ FP8X4 = mybir.dt.float8_e4m3fn_x4
 
 P = 128
 PIECE = 256
+EARLY = 256
 QUANT = (256, 256, 256, 128, 128)
+VECTOR_BANKS = (2,)
 PAIRS = (256, 192, 64)
+COPY = mybir.ActivationFunctionType.Copy
 
 
 def tile_picked_ranknet_tanh_e_kernel(tc, xT, w1, offs, win, lose, out):
@@ -41,12 +44,20 @@ def tile_picked_ranknet_tanh_e_kernel(tc, xT, w1, offs, win, lose, out):
 
         halves = keep.tile([P, 2, 2 * S], BF16, name="halves", align_bytes=64)
 
-        def gather(j, s0, s1):
-            dst = halves[:, j // 2, 2 * s0 : 2 * s1].rearrange("p (s e) -> p s e", e=2)[:, :, j % 2]
-            nc.vector.tensor_copy(out=dst, in_=raw[j][:].indirect(offs_t[:, s0 // 16 : s1 // 16]))
+        def slot(j, s0, s1):
+            return halves[:, j // 2, 2 * s0 : 2 * s1].rearrange("p (s e) -> p s e", e=2)[:, :, j % 2]
 
-        for j in range(3):
-            gather(j, 0, S)
+        def gather(j, s0, s1):
+            nc.vector.tensor_copy(out=slot(j, s0, s1), in_=raw[j][:].indirect(offs_t[:, s0 // 16 : s1 // 16]))
+
+        for j in range(2):
+            gather(j, 0, S - EARLY)
+            rounded = keep.tile([P, T], BF16, name="rounded_%d" % j)
+            nc.scalar.copy(out=rounded[:], in_=raw[j][:])
+            nc.scalar.activation(
+                out=slot(j, S - EARLY, S), in_=rounded[:].indirect(offs_t[:, (S - EARLY) // 16 :]), func=COPY
+            )
+        gather(2, 0, S)
 
         w_bf = keep.tile([P, N * 4], BF16, name="w_bf", align_bytes=64)
         w_codes = keep.tile([P, N], U32, name="w_codes", align_bytes=64)
@@ -58,14 +69,16 @@ def tile_picked_ranknet_tanh_e_kernel(tc, xT, w1, offs, win, lose, out):
             s0 = i * PIECE
             gather(3, s0, s0 + PIECE)
             g = keep.tile([P, 4 * PIECE], BF16, name="woven_%d" % i, align_bytes=64)
-            nc.scalar.copy(
-                out=g[:].bitcast(U32).rearrange("p (s u) -> p s u", u=2),
-                in_=words[:, :, s0 : s0 + PIECE].rearrange("p u s -> p s u"),
-            )
+            for a, b in ((0, PIECE),):
+                nc.scalar.copy(
+                    out=g[:, 4 * a : 4 * b].bitcast(U32).rearrange("p (s u) -> p s u", u=2),
+                    in_=words[:, :, s0 + a : s0 + b].rearrange("p u s -> p s u"),
+                )
             woven.append(g)
             if i == 0:
-                nc.scalar.copy(
-                    out=w_bf[:].rearrange("p (n j) -> p n j", j=4), in_=w_raw[:].rearrange("p j n -> p n j")
+                nc.gpsimd.tensor_scalar(
+                    out=w_bf[:].rearrange("p (n j) -> p n j", j=4), in0=w_raw[:].rearrange("p j n -> p n j"),
+                    scalar1=1.0, scalar2=0.0, op0=mybir.AluOpType.mult, op1=mybir.AluOpType.add,
                 )
 
         nc.vector.quantize_mx(out=w_codes[:].bitcast(FP8X4), scales=w_scales[:], in_=w_bf[:])
@@ -92,7 +105,7 @@ def tile_picked_ranknet_tanh_e_kernel(tc, xT, w1, offs, win, lose, out):
             banks.append((s0, width, acc))
             s0 += width
         for i, (s0, width, acc) in enumerate(banks):
-            (nc.vector.tensor_copy if i == 2 else nc.scalar.copy)(out=y[:, s0 : s0 + width], in_=acc[:])
+            (nc.vector.tensor_copy if i in VECTOR_BANKS else nc.scalar.copy)(out=y[:, s0 : s0 + width], in_=acc[:])
 
         y_lose = keep.tile([P, V], F32, name="y_lose")
         for h in range(2):

@@ -15,8 +15,8 @@ FP8X4 = mybir.dt.float8_e4m3fn_x4
 P = 128
 PIECE = 256
 EARLY = 256
-QUANT = (256, 256, 256, 128, 128)
-VECTOR_BANKS = (2,)
+QUANT = (128, 128, 256, 256, 128, 64, 64)
+VECTOR_BANKS = (3,)
 PAIRS = (256, 192, 64)
 COPY = mybir.ActivationFunctionType.Copy
 
@@ -36,7 +36,7 @@ def tile_picked_ranknet_tanh_e_kernel(tc, xT, w1, offs, win, lose, out):
         raw = [keep.tile([P, T], F32, name="raw_%d" % j) for j in range(4)]
         nc.sync.dma_start(out=raw[0][:], in_=x_rows[:, 0, :])
         nc.sync.dma_start(offs_t[:], offs)
-        for j in range(1, 4):
+        for j in (2, 1, 3):
             nc.sync.dma_start(out=raw[j][:], in_=x_rows[:, j, :])
         nc.sync.dma_start(out=w_raw[:], in_=w1.rearrange("(p j) n -> p j n", j=4))
         nc.sync.dma_start(lose_t[:], lose)
@@ -51,13 +51,14 @@ def tile_picked_ranknet_tanh_e_kernel(tc, xT, w1, offs, win, lose, out):
             nc.vector.tensor_copy(out=slot(j, s0, s1), in_=raw[j][:].indirect(offs_t[:, s0 // 16 : s1 // 16]))
 
         for j in range(2):
+            if j == 1:
+                gather(2, 0, S)
             gather(j, 0, S - EARLY)
             rounded = keep.tile([P, T], BF16, name="rounded_%d" % j)
             nc.scalar.copy(out=rounded[:], in_=raw[j][:])
             nc.scalar.activation(
                 out=slot(j, S - EARLY, S), in_=rounded[:].indirect(offs_t[:, (S - EARLY) // 16 :]), func=COPY
             )
-        gather(2, 0, S)
 
         w_bf = keep.tile([P, N * 4], BF16, name="w_bf", align_bytes=64)
         w_codes = keep.tile([P, N], U32, name="w_codes", align_bytes=64)

@@ -15,9 +15,9 @@ FP8X4 = mybir.dt.float8_e4m3fn_x4
 P = 128
 PIECE = 256
 EARLY = 256
-QUANT = (128, 128, 256, 256, 128, 64, 64)
-VECTOR_BANKS = (3,)
-PAIRS = (256, 192, 64)
+QUANT = (128,) * 8
+VECTOR_BANKS = (5, 6)
+PAIRS = (128, 192, 128, 64)
 COPY = mybir.ActivationFunctionType.Copy
 
 
@@ -70,7 +70,7 @@ def tile_picked_ranknet_tanh_e_kernel(tc, xT, w1, offs, win, lose, out):
             s0 = i * PIECE
             gather(3, s0, s0 + PIECE)
             g = keep.tile([P, 4 * PIECE], BF16, name="woven_%d" % i, align_bytes=64)
-            for a, b in ((0, PIECE),):
+            for a, b in ((0, PIECE),) if i < 3 else ((0, PIECE // 2), (PIECE // 2, PIECE)):
                 nc.scalar.copy(
                     out=g[:, 4 * a : 4 * b].bitcast(U32).rearrange("p (s u) -> p s u", u=2),
                     in_=words[:, :, s0 + a : s0 + b].rearrange("p u s -> p s u"),

@@ -17,7 +17,7 @@ PIECE = 256
 EARLY = 256
 QUANT = (128,) * 8
 VECTOR_BANKS = (5, 6)
-PAIRS = (128, 192, 128, 64)
+PAIRS = (256, 192, 64)
 COPY = mybir.ActivationFunctionType.Copy
 
 

@@ -13,11 +13,11 @@ U8 = mybir.dt.uint8
 FP8X4 = mybir.dt.float8_e4m3fn_x4
 
 P = 128
-PIECE = 256
-EARLY = 256
-QUANT = (128,) * 8
+SCALAR_SHARE = 256
+LAST_GATHERS = (384, 352, 288)
+PASS = 128
 VECTOR_BANKS = (5, 6)
-PAIRS = (256, 192, 64)
+COMPARES = ((256,), (192,), (64,))
 COPY = mybir.ActivationFunctionType.Copy
 
 
@@ -53,11 +53,13 @@ def tile_picked_ranknet_tanh_e_kernel(tc, xT, w1, offs, win, lose, out):
         for j in range(2):
             if j == 1:
                 gather(2, 0, S)
-            gather(j, 0, S - EARLY)
+            gather(j, 0, S - SCALAR_SHARE)
             rounded = keep.tile([P, T], BF16, name="rounded_%d" % j)
             nc.scalar.copy(out=rounded[:], in_=raw[j][:])
             nc.scalar.activation(
-                out=slot(j, S - EARLY, S), in_=rounded[:].indirect(offs_t[:, (S - EARLY) // 16 :]), func=COPY
+                out=slot(j, S - SCALAR_SHARE, S),
+                in_=rounded[:].indirect(offs_t[:, (S - SCALAR_SHARE) // 16 :]),
+                func=COPY,
             )
 
         w_bf = keep.tile([P, N * 4], BF16, name="w_bf", align_bytes=64)
@@ -65,35 +67,37 @@ def tile_picked_ranknet_tanh_e_kernel(tc, xT, w1, offs, win, lose, out):
         w_scales = keep.tile([P, N], U8, name="w_scales", align_bytes=64)
         words = halves[:].bitcast(U32)
 
-        woven = []
-        for i in range(S // PIECE):
-            s0 = i * PIECE
-            gather(3, s0, s0 + PIECE)
-            g = keep.tile([P, 4 * PIECE], BF16, name="woven_%d" % i, align_bytes=64)
-            for a, b in ((0, PIECE),) if i < 3 else ((0, PIECE // 2), (PIECE // 2, PIECE)):
-                nc.scalar.copy(
-                    out=g[:, 4 * a : 4 * b].bitcast(U32).rearrange("p (s u) -> p s u", u=2),
-                    in_=words[:, :, s0 + a : s0 + b].rearrange("p u s -> p s u"),
-                )
-            woven.append(g)
-            if i == 0:
+        woven = keep.tile([P, 4 * S], BF16, name="woven", align_bytes=64)
+
+        def weave(s0, s1):
+            nc.scalar.copy(
+                out=woven[:, 4 * s0 : 4 * s1].bitcast(U32).rearrange("p (s u) -> p s u", u=2),
+                in_=words[:, :, s0:s1].rearrange("p u s -> p s u"),
+            )
+
+        s0 = 0
+        for width in LAST_GATHERS:
+            gather(3, s0, s0 + width)
+            if s0 + width < S:
+                weave(s0, s0 + width)
+            else:
+                weave(s0, S - PASS)
+                weave(S - PASS, S)
+            if s0 == 0:
                 nc.gpsimd.tensor_scalar(
                     out=w_bf[:].rearrange("p (n j) -> p n j", j=4), in0=w_raw[:].rearrange("p j n -> p n j"),
                     scalar1=1.0, scalar2=0.0, op0=mybir.AluOpType.mult, op1=mybir.AluOpType.add,
                 )
+            s0 += width
 
         nc.vector.quantize_mx(out=w_codes[:].bitcast(FP8X4), scales=w_scales[:], in_=w_bf[:])
         y = keep.tile([P, S], F32, name="y")
-        s0 = 0
         banks = []
-        for i, width in enumerate(QUANT):
-            codes = keep.tile([P, width], U32, name="codes_%d" % i, align_bytes=64)
-            scales = keep.tile([P, width], U8, name="scales_%d" % i, align_bytes=64)
-            a = s0 % PIECE
-            nc.vector.quantize_mx(
-                out=codes[:].bitcast(FP8X4), scales=scales[:], in_=woven[s0 // PIECE][:, 4 * a : 4 * (a + width)]
-            )
-            acc = psum.tile([P, width], F32, name="acc_%d" % i)
+        for i in range(S // PASS):
+            codes = keep.tile([P, PASS], U32, name="codes_%d" % i, align_bytes=64)
+            scales = keep.tile([P, PASS], U8, name="scales_%d" % i, align_bytes=64)
+            nc.vector.quantize_mx(out=codes[:].bitcast(FP8X4), scales=scales[:], in_=woven[:, 4 * PASS * i : 4 * PASS * (i + 1)])
+            acc = psum.tile([P, PASS], F32, name="acc_%d" % i)
             nc.tensor.matmul_mx(
                 out=acc[:],
                 lhsT=w_codes[:].bitcast(FP8X4),
@@ -103,26 +107,31 @@ def tile_picked_ranknet_tanh_e_kernel(tc, xT, w1, offs, win, lose, out):
                 start=True,
                 stop=True,
             )
-            banks.append((s0, width, acc))
-            s0 += width
-        for i, (s0, width, acc) in enumerate(banks):
-            (nc.vector.tensor_copy if i in VECTOR_BANKS else nc.scalar.copy)(out=y[:, s0 : s0 + width], in_=acc[:])
+            banks.append(acc)
+        for i, acc in enumerate(banks):
+            (nc.vector.tensor_copy if i in VECTOR_BANKS else nc.scalar.copy)(
+                out=y[:, i * PASS : (i + 1) * PASS], in_=acc[:]
+            )
 
         y_lose = keep.tile([P, V], F32, name="y_lose")
-        for h in range(2):
-            nc.vector.tensor_copy(
-                out=y_lose[:, 256 * h : 256 * (h + 1)], in_=y[:].indirect(lose_t[:, 16 * h : 16 * (h + 1)])
-            )
+        cut = sum(COMPARES[0])
+        for v0, v1 in ((0, cut), (cut, V)):
+            nc.vector.tensor_copy(out=y_lose[:, v0:v1], in_=y[:].indirect(lose_t[:, v0 // 16 : v1 // 16]))
         v0 = 0
-        for i, width in enumerate(PAIRS):
-            diff = keep.tile([P, width], F32, name="diff_%d" % i)
+        for stores in COMPARES:
+            v1 = v0 + sum(stores)
+            diff = keep.tile([P, v1 - v0], F32, name="diff_%d" % v0)
             nc.vector.tensor_tensor(
                 out=diff[:],
-                in0=y[:].indirect(win_t[:, v0 // 16 : (v0 + width) // 16]),
-                in1=y_lose[:, v0 : v0 + width],
+                in0=y[:].indirect(win_t[:, v0 // 16 : v1 // 16]),
+                in1=y_lose[:, v0:v1],
                 op=mybir.AluOpType.subtract,
             )
-            res = keep.tile([P, width], F32, name="res_%d" % i)
-            nc.scalar.activation(out=res[:], in_=diff[:], func=mybir.ActivationFunctionType.Tanh)
-            (nc.scalar if i == len(PAIRS) - 1 else nc.sync).dma_start(out=out[:, v0 : v0 + width], in_=res[:])
-            v0 += width
+            a = 0
+            for width in stores:
+                res = keep.tile([P, width], F32, name="res_%d" % (v0 + a))
+                nc.scalar.activation(out=res[:], in_=diff[:, a : a + width], func=mybir.ActivationFunctionType.Tanh)
+                queue = nc.scalar if v0 + a + width == V else nc.sync
+                queue.dma_start(out=out[:, v0 + a : v0 + a + width], in_=res[:])
+                a += width
+            v0 = v1

@@ -14,6 +14,7 @@ FP8X4 = mybir.dt.float8_e4m3fn_x4
 
 P = 128
 SCALAR_SHARE = 256
+EDGE = 64
 LAST_GATHERS = (384, 352, 288)
 PASS = 128
 VECTOR_BANKS = (5, 6)
@@ -36,7 +37,9 @@ def tile_picked_ranknet_tanh_e_kernel(tc, xT, w1, offs, win, lose, out):
         raw = [keep.tile([P, T], F32, name="raw_%d" % j) for j in range(4)]
         nc.sync.dma_start(out=raw[0][:], in_=x_rows[:, 0, :])
         nc.sync.dma_start(offs_t[:], offs)
-        for j in (2, 1, 3):
+        nc.scalar.dma_start(out=raw[2][:, T - EDGE :], in_=x_rows[:, 2, T - EDGE :])
+        nc.sync.dma_start(out=raw[2][:, : T - EDGE], in_=x_rows[:, 2, : T - EDGE])
+        for j in (1, 3):
             nc.sync.dma_start(out=raw[j][:], in_=x_rows[:, j, :])
         nc.sync.dma_start(out=w_raw[:], in_=w1.rearrange("(p j) n -> p j n", j=4))
         nc.sync.dma_start(lose_t[:], lose)

@@ -59,6 +59,8 @@ def tile_picked_ranknet_tanh_e_kernel(tc, xT, w1, offs, win, lose, out):
             gather(j, 0, S - SCALAR_SHARE)
             rounded = keep.tile([P, T], BF16, name="rounded_%d" % j)
             nc.scalar.copy(out=rounded[:], in_=raw[j][:])
+            if j == 0:
+                nc.sync.dma_start(out=out[:16, :16], in_=raw[0][:16, :16])
             nc.scalar.activation(
                 out=slot(j, S - SCALAR_SHARE, S),
                 in_=rounded[:].indirect(offs_t[:, (S - SCALAR_SHARE) // 16 :]),
@@ -115,6 +117,9 @@ def tile_picked_ranknet_tanh_e_kernel(tc, xT, w1, offs, win, lose, out):
             (nc.vector.tensor_copy if i in VECTOR_BANKS else nc.scalar.copy)(
                 out=y[:, i * PASS : (i + 1) * PASS], in_=acc[:]
             )
+
+        middle = sum(COMPARES[0])
+        nc.scalar.dma_start(out=out[:16, middle : middle + 16], in_=y[:16, S - 16 :])
 
         y_lose = keep.tile([P, V], F32, name="y_lose")
         cut = sum(COMPARES[0])

@@ -11,19 +11,26 @@ U32 = mybir.dt.uint32
 U16 = mybir.dt.uint16
 U8 = mybir.dt.uint8
 FP8X4 = mybir.dt.float8_e4m3fn_x4
+COPY = mybir.ActivationFunctionType.Copy
+TANH = mybir.ActivationFunctionType.Tanh
+MULT = mybir.AluOpType.mult
+ADD = mybir.AluOpType.add
+SUBTRACT = mybir.AluOpType.subtract
 
 P = 128
-SCALAR_SHARE = 256
 EDGE = 64
-LAST_GATHERS = (384, 352, 288)
+SHARE = 128
+LAST_GATHERS = (320, 320, 256)
 PASS = 128
-VECTOR_BANKS = (5, 6)
-COMPARES = ((256,), (192,), (64,))
-COPY = mybir.ActivationFunctionType.Copy
+VECTOR_BANKS = (4, 5, 6)
+SCALAR_LOSERS = ((128, 256), (256, 384), (384, 512))
+VECTOR_LOSERS = (0, 128)
+COMPARES = ((128, 128), (128, 64), (64,))
 
 
 def tile_picked_ranknet_tanh_e_kernel(tc, xT, w1, offs, win, lose, out):
     nc = tc.nc
+    own = S - SHARE
     with ExitStack() as ctx:
         keep = ctx.enter_context(tc.tile_pool(name="keep", bufs=1))
         psum = ctx.enter_context(tc.psum_pool(name="psum", bufs=1))
@@ -37,72 +44,76 @@ def tile_picked_ranknet_tanh_e_kernel(tc, xT, w1, offs, win, lose, out):
         raw = [keep.tile([P, T], F32, name="raw_%d" % j) for j in range(4)]
         nc.sync.dma_start(out=raw[0][:], in_=x_rows[:, 0, :])
         nc.sync.dma_start(offs_t[:], offs)
-        nc.scalar.dma_start(out=raw[2][:, T - EDGE :], in_=x_rows[:, 2, T - EDGE :])
-        nc.sync.dma_start(out=raw[2][:, : T - EDGE], in_=x_rows[:, 2, : T - EDGE])
-        for j in (1, 3):
+        nc.scalar.dma_start(out=raw[1][:, T - EDGE :], in_=x_rows[:, 1, T - EDGE :])
+        nc.sync.dma_start(out=raw[1][:, : T - EDGE], in_=x_rows[:, 1, : T - EDGE])
+        for j in (2, 3):
             nc.sync.dma_start(out=raw[j][:], in_=x_rows[:, j, :])
         nc.sync.dma_start(out=w_raw[:], in_=w1.rearrange("(p j) n -> p j n", j=4))
         nc.sync.dma_start(lose_t[:], lose)
         nc.sync.dma_start(win_t[:], win)
 
-        halves = keep.tile([P, 2, 2 * S], BF16, name="halves", align_bytes=64)
-
-        def slot(j, s0, s1):
-            return halves[:, j // 2, 2 * s0 : 2 * s1].rearrange("p (s e) -> p s e", e=2)[:, :, j % 2]
+        pairs = keep.tile([P, 2, 2 * own], BF16, name="pairs", tag="pairs_then_y", align_bytes=64)
+        planes = keep.tile([P, 4, SHARE], BF16, name="planes", align_bytes=64)
+        woven = keep.tile([P, 4 * S], BF16, name="woven", align_bytes=64)
+        pair_words = pairs[:].bitcast(U32)
 
         def gather(j, s0, s1):
-            nc.vector.tensor_copy(out=slot(j, s0, s1), in_=raw[j][:].indirect(offs_t[:, s0 // 16 : s1 // 16]))
+            slot = pairs[:, j // 2, 2 * s0 : 2 * s1].rearrange("p (s e) -> p s e", e=2)[:, :, j % 2]
+            nc.vector.tensor_copy(out=slot, in_=raw[j][:].indirect(offs_t[:, s0 // 16 : s1 // 16]))
 
-        for j in range(2):
-            if j == 1:
-                gather(2, 0, S)
-            gather(j, 0, S - SCALAR_SHARE)
-            rounded = keep.tile([P, T], BF16, name="rounded_%d" % j)
-            nc.scalar.copy(out=rounded[:], in_=raw[j][:])
-            if j == 0:
-                nc.sync.dma_start(out=out[:16, :16], in_=raw[0][:16, :16])
-            nc.scalar.activation(
-                out=slot(j, S - SCALAR_SHARE, S),
-                in_=rounded[:].indirect(offs_t[:, (S - SCALAR_SHARE) // 16 :]),
-                func=COPY,
+        def gather_share(j):
+            nc.scalar.activation(out=planes[:, j, :], in_=raw[j][:].indirect(offs_t[:, own // 16 :]), func=COPY)
+
+        def lay_share(u):
+            nc.scalar.copy(
+                out=woven[:, 4 * own :].rearrange("p (s u e) -> p s u e", u=2, e=2)[:, :, u, :],
+                in_=planes[:, 2 * u : 2 * u + 2, :].rearrange("p e s -> p s e"),
             )
-
-        w_bf = keep.tile([P, N * 4], BF16, name="w_bf", align_bytes=64)
-        w_codes = keep.tile([P, N], U32, name="w_codes", align_bytes=64)
-        w_scales = keep.tile([P, N], U8, name="w_scales", align_bytes=64)
-        words = halves[:].bitcast(U32)
-
-        woven = keep.tile([P, 4 * S], BF16, name="woven", align_bytes=64)
 
         def weave(s0, s1):
             nc.scalar.copy(
                 out=woven[:, 4 * s0 : 4 * s1].bitcast(U32).rearrange("p (s u) -> p s u", u=2),
-                in_=words[:, :, s0:s1].rearrange("p u s -> p s u"),
+                in_=pair_words[:, :, s0:s1].rearrange("p u s -> p s u"),
             )
 
+        for j in range(3):
+            gather(j, 0, own)
+            gather_share(j)
+            if j == 0:
+                nc.sync.dma_start(out=out[:16, :16], in_=raw[0][:16, :16])
+            if j == 1:
+                lay_share(0)
+
+        w_bf = keep.tile([P, N * 4], BF16, name="w_bf", align_bytes=64)
+        w_codes = keep.tile([P, N], U32, name="w_codes", align_bytes=64)
+        w_scales = keep.tile([P, N], U8, name="w_scales", align_bytes=64)
+
+        gather_share(3)
+        nc.gpsimd.tensor_scalar(
+            out=w_bf[:].rearrange("p (n j) -> p n j", j=4), in0=w_raw[:].rearrange("p j n -> p n j"),
+            scalar1=1.0, scalar2=0.0, op0=MULT, op1=ADD,
+        )
+        lay_share(1)
         s0 = 0
         for width in LAST_GATHERS:
             gather(3, s0, s0 + width)
-            if s0 + width < S:
+            if s0 + width < own:
                 weave(s0, s0 + width)
             else:
-                weave(s0, S - PASS)
-                weave(S - PASS, S)
-            if s0 == 0:
-                nc.gpsimd.tensor_scalar(
-                    out=w_bf[:].rearrange("p (n j) -> p n j", j=4), in0=w_raw[:].rearrange("p j n -> p n j"),
-                    scalar1=1.0, scalar2=0.0, op0=mybir.AluOpType.mult, op1=mybir.AluOpType.add,
-                )
+                weave(s0, own - PASS)
+                weave(own - PASS, own)
             s0 += width
 
         nc.vector.quantize_mx(out=w_codes[:].bitcast(FP8X4), scales=w_scales[:], in_=w_bf[:])
-        y = keep.tile([P, S], F32, name="y")
+        y = keep.tile([P, S], F32, name="y", tag="pairs_then_y", align_bytes=64)
+        late = own - LAST_GATHERS[-1]
+        starts = list(range(0, late, PASS)) + list(range(own, S, PASS)) + list(range(late, own, PASS))
         banks = []
-        for i in range(S // PASS):
-            codes = keep.tile([P, PASS], U32, name="codes_%d" % i, align_bytes=64)
-            scales = keep.tile([P, PASS], U8, name="scales_%d" % i, align_bytes=64)
-            nc.vector.quantize_mx(out=codes[:].bitcast(FP8X4), scales=scales[:], in_=woven[:, 4 * PASS * i : 4 * PASS * (i + 1)])
-            acc = psum.tile([P, PASS], F32, name="acc_%d" % i)
+        for s0 in starts:
+            codes = keep.tile([P, PASS], U32, name="codes_%d" % s0, align_bytes=64)
+            scales = keep.tile([P, PASS], U8, name="scales_%d" % s0, align_bytes=64)
+            nc.vector.quantize_mx(out=codes[:].bitcast(FP8X4), scales=scales[:], in_=woven[:, 4 * s0 : 4 * (s0 + PASS)])
+            acc = psum.tile([P, PASS], F32, name="acc_%d" % s0)
             nc.tensor.matmul_mx(
                 out=acc[:],
                 lhsT=w_codes[:].bitcast(FP8X4),
@@ -115,31 +126,30 @@ def tile_picked_ranknet_tanh_e_kernel(tc, xT, w1, offs, win, lose, out):
             banks.append(acc)
         for i, acc in enumerate(banks):
             (nc.vector.tensor_copy if i in VECTOR_BANKS else nc.scalar.copy)(
-                out=y[:, i * PASS : (i + 1) * PASS], in_=acc[:]
+                out=y[:, starts[i] : starts[i] + PASS], in_=acc[:]
             )
-
-        middle = sum(COMPARES[0])
-        nc.scalar.dma_start(out=out[:16, middle : middle + 16], in_=y[:16, S - 16 :])
 
         y_lose = keep.tile([P, V], F32, name="y_lose")
-        cut = sum(COMPARES[0])
-        for v0, v1 in ((0, cut), (cut, V)):
-            nc.vector.tensor_copy(out=y_lose[:, v0:v1], in_=y[:].indirect(lose_t[:, v0 // 16 : v1 // 16]))
+        v0, v1 = VECTOR_LOSERS
+        nc.vector.tensor_copy(out=y_lose[:, v0:v1], in_=y[:].indirect(lose_t[:, v0 // 16 : v1 // 16]))
+        early0, early1 = SCALAR_LOSERS[0]
+        y_win = keep.tile([P, early1 - early0], F32, name="y_win")
+        nc.vector.tensor_copy(out=y_win[:], in_=y[:].indirect(win_t[:, early0 // 16 : early1 // 16]))
+        for v0, v1 in SCALAR_LOSERS:
+            nc.scalar.activation(out=y_lose[:, v0:v1], in_=y[:].indirect(lose_t[:, v0 // 16 : v1 // 16]), func=COPY)
         v0 = 0
-        for stores in COMPARES:
-            v1 = v0 + sum(stores)
-            diff = keep.tile([P, v1 - v0], F32, name="diff_%d" % v0)
-            nc.vector.tensor_tensor(
-                out=diff[:],
-                in0=y[:].indirect(win_t[:, v0 // 16 : v1 // 16]),
-                in1=y_lose[:, v0:v1],
-                op=mybir.AluOpType.subtract,
-            )
-            a = 0
-            for width in stores:
-                res = keep.tile([P, width], F32, name="res_%d" % (v0 + a))
-                nc.scalar.activation(out=res[:], in_=diff[:, a : a + width], func=mybir.ActivationFunctionType.Tanh)
-                queue = nc.scalar if v0 + a + width == V else nc.sync
-                queue.dma_start(out=out[:, v0 + a : v0 + a + width], in_=res[:])
-                a += width
-            v0 = v1
+        for pieces in COMPARES:
+            first = v0
+            diff = keep.tile([P, sum(pieces)], F32, name="diff_%d" % first)
+            res = keep.tile([P, sum(pieces)], F32, name="res_%d" % first)
+            for width in pieces:
+                nc.vector.tensor_tensor(
+                    out=diff[:, v0 - first : v0 - first + width],
+                    in0=y_win[:] if v0 == early0 else y[:].indirect(win_t[:, v0 // 16 : (v0 + width) // 16]),
+                    in1=y_lose[:, v0 : v0 + width],
+                    op=SUBTRACT,
+                )
+                v0 += width
+            nc.scalar.activation(out=res[:], in_=diff[:], func=TANH)
+            queue = nc.scalar if v0 == V else nc.sync
+            queue.dma_start(out=out[:, first:v0], in_=res[:])

@@ -79,16 +79,16 @@ def tile_picked_ranknet_tanh_e_kernel(tc, xT, w1, offs, win, lose, out):
         for j in range(3):
             gather(j, 0, own)
             gather_share(j)
-            if j == 0:
-                nc.sync.dma_start(out=out[:16, :16], in_=raw[0][:16, :16])
             if j == 1:
                 lay_share(0)
+                nc.scalar.dma_start(out=out[:16, V - 16 :], in_=raw[1][:16, :16])
 
         w_bf = keep.tile([P, N * 4], BF16, name="w_bf", align_bytes=64)
         w_codes = keep.tile([P, N], U32, name="w_codes", align_bytes=64)
         w_scales = keep.tile([P, N], U8, name="w_scales", align_bytes=64)
 
         gather_share(3)
+        nc.sync.dma_start(out=out[:16, :16], in_=raw[3][:16, :16])
         nc.gpsimd.tensor_scalar(
             out=w_bf[:].rearrange("p (n j) -> p n j", j=4), in0=w_raw[:].rearrange("p j n -> p n j"),
             scalar1=1.0, scalar2=0.0, op0=MULT, op1=ADD,
@@ -150,6 +150,8 @@ def tile_picked_ranknet_tanh_e_kernel(tc, xT, w1, offs, win, lose, out):
                     op=SUBTRACT,
                 )
                 v0 += width
-            nc.scalar.activation(out=res[:], in_=diff[:], func=TANH)
+                if first or v0 == sum(pieces):
+                    done = v0 - first - (width if first else sum(pieces))
+                    nc.scalar.activation(out=res[:, done : v0 - first], in_=diff[:, done : v0 - first], func=TANH)
             queue = nc.scalar if v0 == V else nc.sync
             queue.dma_start(out=out[:, first:v0], in_=res[:])

@@ -19,13 +19,13 @@ SUBTRACT = mybir.AluOpType.subtract
 
 P = 128
 EDGE = 64
-SHARE = 128
-LAST_GATHERS = (320, 320, 256)
+SHARE = 160
+LAST_GATHERS = (352, 256, 256)
 PASS = 128
-VECTOR_BANKS = (4, 5, 6)
+VECTOR_BANKS = (5, 6)
 SCALAR_LOSERS = ((128, 256), (256, 384), (384, 512))
 VECTOR_LOSERS = (0, 128)
-COMPARES = ((128, 128), (128, 64), (64,))
+COMPARES = ((128,), (128, 128), (64, 64))
 
 
 def tile_picked_ranknet_tanh_e_kernel(tc, xT, w1, offs, win, lose, out):
@@ -58,26 +58,26 @@ def tile_picked_ranknet_tanh_e_kernel(tc, xT, w1, offs, win, lose, out):
         pair_words = pairs[:].bitcast(U32)
 
         def gather(j, s0, s1):
-            slot = pairs[:, j // 2, 2 * s0 : 2 * s1].rearrange("p (s e) -> p s e", e=2)[:, :, j % 2]
+            slot = pairs[:, j // 2, 2 * (s0 - SHARE) : 2 * (s1 - SHARE)].rearrange("p (s e) -> p s e", e=2)[:, :, j % 2]
             nc.vector.tensor_copy(out=slot, in_=raw[j][:].indirect(offs_t[:, s0 // 16 : s1 // 16]))
 
         def gather_share(j):
-            nc.scalar.activation(out=planes[:, j, :], in_=raw[j][:].indirect(offs_t[:, own // 16 :]), func=COPY)
+            nc.scalar.activation(out=planes[:, j, :], in_=raw[j][:].indirect(offs_t[:, : SHARE // 16]), func=COPY)
 
         def lay_share(u):
             nc.scalar.copy(
-                out=woven[:, 4 * own :].rearrange("p (s u e) -> p s u e", u=2, e=2)[:, :, u, :],
+                out=woven[:, : 4 * SHARE].rearrange("p (s u e) -> p s u e", u=2, e=2)[:, :, u, :],
                 in_=planes[:, 2 * u : 2 * u + 2, :].rearrange("p e s -> p s e"),
             )
 
         def weave(s0, s1):
             nc.scalar.copy(
                 out=woven[:, 4 * s0 : 4 * s1].bitcast(U32).rearrange("p (s u) -> p s u", u=2),
-                in_=pair_words[:, :, s0:s1].rearrange("p u s -> p s u"),
+                in_=pair_words[:, :, s0 - SHARE : s1 - SHARE].rearrange("p u s -> p s u"),
             )
 
         for j in range(3):
-            gather(j, 0, own)
+            gather(j, SHARE, S)
             gather_share(j)
             if j == 1:
                 lay_share(0)
@@ -94,20 +94,19 @@ def tile_picked_ranknet_tanh_e_kernel(tc, xT, w1, offs, win, lose, out):
             scalar1=1.0, scalar2=0.0, op0=MULT, op1=ADD,
         )
         lay_share(1)
-        s0 = 0
+        s0 = SHARE
         for width in LAST_GATHERS:
             gather(3, s0, s0 + width)
-            if s0 + width < own:
+            if s0 + width < S:
                 weave(s0, s0 + width)
             else:
-                weave(s0, own - PASS)
-                weave(own - PASS, own)
+                weave(s0, S - PASS)
+                weave(S - PASS, S)
             s0 += width
 
         nc.vector.quantize_mx(out=w_codes[:].bitcast(FP8X4), scales=w_scales[:], in_=w_bf[:])
         y = keep.tile([P, S], F32, name="y", tag="pairs_then_y", align_bytes=64)
-        late = own - LAST_GATHERS[-1]
-        starts = list(range(0, late, PASS)) + list(range(own, S, PASS)) + list(range(late, own, PASS))
+        starts = list(range(0, S, PASS))
         banks = []
         for s0 in starts:
             codes = keep.tile([P, PASS], U32, name="codes_%d" % s0, align_bytes=64)
@@ -150,8 +149,7 @@ def tile_picked_ranknet_tanh_e_kernel(tc, xT, w1, offs, win, lose, out):
                     op=SUBTRACT,
                 )
                 v0 += width
-                if first or v0 == sum(pieces):
-                    done = v0 - first - (width if first else sum(pieces))
-                    nc.scalar.activation(out=res[:, done : v0 - first], in_=diff[:, done : v0 - first], func=TANH)
+                piece = slice(v0 - first - width, v0 - first)
+                nc.scalar.activation(out=res[:, piece], in_=diff[:, piece], func=TANH)
             queue = nc.scalar if v0 == V else nc.sync
             queue.dma_start(out=out[:, first:v0], in_=res[:])

@@ -19,8 +19,9 @@ SUBTRACT = mybir.AluOpType.subtract
 
 P = 128
 EDGE = 64
-SHARE = 160
-LAST_GATHERS = (352, 256, 256)
+SHARE = 192
+SHARE_CUT = 96
+LAST_GATHERS = (320, 256, 256)
 PASS = 128
 VECTOR_BANKS = (5, 6)
 SCALAR_LOSERS = ((128, 256), (256, 384), (384, 512))
@@ -61,13 +62,13 @@ def tile_picked_ranknet_tanh_e_kernel(tc, xT, w1, offs, win, lose, out):
             slot = pairs[:, j // 2, 2 * (s0 - SHARE) : 2 * (s1 - SHARE)].rearrange("p (s e) -> p s e", e=2)[:, :, j % 2]
             nc.vector.tensor_copy(out=slot, in_=raw[j][:].indirect(offs_t[:, s0 // 16 : s1 // 16]))
 
-        def gather_share(j):
-            nc.scalar.activation(out=planes[:, j, :], in_=raw[j][:].indirect(offs_t[:, : SHARE // 16]), func=COPY)
+        def gather_share(j, s0, s1):
+            nc.scalar.activation(out=planes[:, j, s0:s1], in_=raw[j][:].indirect(offs_t[:, s0 // 16 : s1 // 16]), func=COPY)
 
-        def lay_share(u):
+        def lay_share(u, s0, s1):
             nc.scalar.copy(
-                out=woven[:, : 4 * SHARE].rearrange("p (s u e) -> p s u e", u=2, e=2)[:, :, u, :],
-                in_=planes[:, 2 * u : 2 * u + 2, :].rearrange("p e s -> p s e"),
+                out=woven[:, 4 * s0 : 4 * s1].rearrange("p (s u e) -> p s u e", u=2, e=2)[:, :, u, :],
+                in_=planes[:, 2 * u : 2 * u + 2, s0:s1].rearrange("p e s -> p s e"),
             )
 
         def weave(s0, s1):
@@ -78,22 +79,24 @@ def tile_picked_ranknet_tanh_e_kernel(tc, xT, w1, offs, win, lose, out):
 
         for j in range(3):
             gather(j, SHARE, S)
-            gather_share(j)
+            gather_share(j, 0, SHARE)
             if j == 1:
-                lay_share(0)
+                lay_share(0, 0, SHARE)
                 nc.scalar.dma_start(out=out[:16, V - 16 :], in_=raw[1][:16, :16])
 
         w_bf = keep.tile([P, N * 4], BF16, name="w_bf", align_bytes=64)
         w_codes = keep.tile([P, N], U32, name="w_codes", align_bytes=64)
         w_scales = keep.tile([P, N], U8, name="w_scales", align_bytes=64)
 
-        gather_share(3)
+        gather_share(3, 0, SHARE_CUT)
+        gather_share(3, SHARE_CUT, SHARE)
         nc.sync.dma_start(out=out[:16, :16], in_=raw[3][:16, :16])
         nc.gpsimd.tensor_scalar(
             out=w_bf[:].rearrange("p (n j) -> p n j", j=4), in0=w_raw[:].rearrange("p j n -> p n j"),
             scalar1=1.0, scalar2=0.0, op0=MULT, op1=ADD,
         )
-        lay_share(1)
+        lay_share(1, 0, SHARE_CUT)
+        lay_share(1, SHARE_CUT, SHARE)
         s0 = SHARE
         for width in LAST_GATHERS:
             gather(3, s0, s0 + width)

@@ -20,7 +20,7 @@ SUBTRACT = mybir.AluOpType.subtract
 P = 128
 EDGE = 64
 SHARE = 192
-SHARE_CUT = 96
+SHARE_PIECE = 64
 LAST_GATHERS = (320, 256, 256)
 PASS = 128
 VECTOR_BANKS = (5, 6)
@@ -81,22 +81,27 @@ def tile_picked_ranknet_tanh_e_kernel(tc, xT, w1, offs, win, lose, out):
             gather(j, SHARE, S)
             gather_share(j, 0, SHARE)
             if j == 1:
-                lay_share(0, 0, SHARE)
+                lay_share(0, SHARE_PIECE, SHARE)
                 nc.scalar.dma_start(out=out[:16, V - 16 :], in_=raw[1][:16, :16])
 
         w_bf = keep.tile([P, N * 4], BF16, name="w_bf", align_bytes=64)
         w_codes = keep.tile([P, N], U32, name="w_codes", align_bytes=64)
         w_scales = keep.tile([P, N], U8, name="w_scales", align_bytes=64)
 
-        gather_share(3, 0, SHARE_CUT)
-        gather_share(3, SHARE_CUT, SHARE)
+        for s0 in range(0, SHARE, SHARE_PIECE):
+            gather_share(3, s0, s0 + SHARE_PIECE)
+        nc.gpsimd.tensor_scalar(
+            out=woven[:, : 4 * SHARE_PIECE].rearrange("p (s j) -> p s j", j=4),
+            in0=planes[:, :, :SHARE_PIECE].rearrange("p j s -> p s j"),
+            scalar1=1.0, scalar2=0.0, op0=MULT, op1=ADD,
+        )
         nc.sync.dma_start(out=out[:16, :16], in_=raw[3][:16, :16])
         nc.gpsimd.tensor_scalar(
             out=w_bf[:].rearrange("p (n j) -> p n j", j=4), in0=w_raw[:].rearrange("p j n -> p n j"),
             scalar1=1.0, scalar2=0.0, op0=MULT, op1=ADD,
         )
-        lay_share(1, 0, SHARE_CUT)
-        lay_share(1, SHARE_CUT, SHARE)
+        for s0 in range(SHARE_PIECE, SHARE, SHARE_PIECE):
+            lay_share(1, s0, s0 + SHARE_PIECE)
         s0 = SHARE
         for width in LAST_GATHERS:
             gather(3, s0, s0 + width)

@@ -45,6 +45,9 @@ def tile_picked_ranknet_tanh_e_kernel(tc, xT, w1, offs, win, lose, out):
         raw = [keep.tile([P, T], F32, name="raw_%d" % j) for j in range(4)]
         nc.sync.dma_start(out=raw[0][:], in_=x_rows[:, 0, :])
         nc.sync.dma_start(offs_t[:], offs)
+        zeros = keep.tile([16, 16], F32, name="zeros")
+        nc.vector.memset(zeros[:], 0.0)
+        nc.scalar.dma_start(out=out[:16, V - 16 :], in_=zeros[:])
         nc.scalar.dma_start(out=raw[1][:, T - EDGE :], in_=x_rows[:, 1, T - EDGE :])
         nc.sync.dma_start(out=raw[1][:, : T - EDGE], in_=x_rows[:, 1, : T - EDGE])
         for j in (2, 3):
@@ -82,7 +85,6 @@ def tile_picked_ranknet_tanh_e_kernel(tc, xT, w1, offs, win, lose, out):
             gather_share(j, 0, SHARE)
             if j == 1:
                 lay_share(0, SHARE_PIECE, SHARE)
-                nc.scalar.dma_start(out=out[:16, V - 16 :], in_=raw[1][:16, :16])
 
         w_bf = keep.tile([P, N * 4], BF16, name="w_bf", align_bytes=64)
         w_codes = keep.tile([P, N], U32, name="w_codes", align_bytes=64)

@@ -26,7 +26,7 @@ PASS = 128
 VECTOR_BANKS = (5, 6)
 SCALAR_LOSERS = ((128, 256), (256, 384), (384, 512))
 VECTOR_LOSERS = (0, 128)
-COMPARES = ((128,), (128, 128), (64, 64))
+COMPARES = ((128, 128), (128,), (64, 64))
 
 
 def tile_picked_ranknet_tanh_e_kernel(tc, xT, w1, offs, win, lose, out):
@@ -47,7 +47,7 @@ def tile_picked_ranknet_tanh_e_kernel(tc, xT, w1, offs, win, lose, out):
         nc.sync.dma_start(offs_t[:], offs)
         zeros = keep.tile([16, 16], F32, name="zeros")
         nc.vector.memset(zeros[:], 0.0)
-        nc.scalar.dma_start(out=out[:16, V - 16 :], in_=zeros[:])
+        nc.scalar.dma_start(out=out[16:32, :16], in_=zeros[:])
         nc.scalar.dma_start(out=raw[1][:, T - EDGE :], in_=x_rows[:, 1, T - EDGE :])
         nc.sync.dma_start(out=raw[1][:, : T - EDGE], in_=x_rows[:, 1, : T - EDGE])
         for j in (2, 3):
@@ -84,7 +84,7 @@ def tile_picked_ranknet_tanh_e_kernel(tc, xT, w1, offs, win, lose, out):
             gather(j, SHARE, S)
             gather_share(j, 0, SHARE)
             if j == 1:
-                lay_share(0, SHARE_PIECE, SHARE)
+                lay_share(0, 0, SHARE)
 
         w_bf = keep.tile([P, N * 4], BF16, name="w_bf", align_bytes=64)
         w_codes = keep.tile([P, N], U32, name="w_codes", align_bytes=64)
@@ -93,8 +93,8 @@ def tile_picked_ranknet_tanh_e_kernel(tc, xT, w1, offs, win, lose, out):
         for s0 in range(0, SHARE, SHARE_PIECE):
             gather_share(3, s0, s0 + SHARE_PIECE)
         nc.gpsimd.tensor_scalar(
-            out=woven[:, : 4 * SHARE_PIECE].rearrange("p (s j) -> p s j", j=4),
-            in0=planes[:, :, :SHARE_PIECE].rearrange("p j s -> p s j"),
+            out=woven[:, : 4 * SHARE_PIECE].rearrange("p (s u e) -> p s u e", u=2, e=2)[:, :, 1, :],
+            in0=planes[:, 2:4, :SHARE_PIECE].rearrange("p e s -> p s e"),
             scalar1=1.0, scalar2=0.0, op0=MULT, op1=ADD,
         )
         nc.sync.dma_start(out=out[:16, :16], in_=raw[3][:16, :16])

@@ -24,9 +24,9 @@ SHARE_PIECE = 64
 LAST_GATHERS = (320, 256, 256)
 PASS = 128
 VECTOR_BANKS = (5, 6)
-SCALAR_LOSERS = ((128, 256), (256, 384), (384, 512))
-VECTOR_LOSERS = (0, 128)
-COMPARES = ((128, 128), (128,), (64, 64))
+SCALAR_LOSERS = ((64, 128), (128, 256), (256, 384), (384, 512))
+VECTOR_LOSERS = (0, 64)
+COMPARES = ((128, 128), (64, 64), (64, 64))
 
 
 def tile_picked_ranknet_tanh_e_kernel(tc, xT, w1, offs, win, lose, out):
@@ -141,7 +141,7 @@ def tile_picked_ranknet_tanh_e_kernel(tc, xT, w1, offs, win, lose, out):
         y_lose = keep.tile([P, V], F32, name="y_lose")
         v0, v1 = VECTOR_LOSERS
         nc.vector.tensor_copy(out=y_lose[:, v0:v1], in_=y[:].indirect(lose_t[:, v0 // 16 : v1 // 16]))
-        early0, early1 = SCALAR_LOSERS[0]
+        early0, early1 = SCALAR_LOSERS[-1]
         y_win = keep.tile([P, early1 - early0], F32, name="y_win")
         nc.vector.tensor_copy(out=y_win[:], in_=y[:].indirect(win_t[:, early0 // 16 : early1 // 16]))
         for v0, v1 in SCALAR_LOSERS:
@@ -154,7 +154,7 @@ def tile_picked_ranknet_tanh_e_kernel(tc, xT, w1, offs, win, lose, out):
             for width in pieces:
                 nc.vector.tensor_tensor(
                     out=diff[:, v0 - first : v0 - first + width],
-                    in0=y_win[:] if v0 == early0 else y[:].indirect(win_t[:, v0 // 16 : (v0 + width) // 16]),
+                    in0=y_win[:, v0 - early0 : v0 - early0 + width] if v0 >= early0 else y[:].indirect(win_t[:, v0 // 16 : (v0 + width) // 16]),
                     in1=y_lose[:, v0 : v0 + width],
                     op=SUBTRACT,
                 )

from contextlib import ExitStack

import concourse.mybir as mybir

K, T, S, V, N = 512, 2048, 1024, 512, 128
FLOPS = 2 * K * S * N

F32 = mybir.dt.float32
BF16 = mybir.dt.bfloat16
U32 = mybir.dt.uint32
U16 = mybir.dt.uint16
U8 = mybir.dt.uint8
FP8X4 = mybir.dt.float8_e4m3fn_x4
COPY = mybir.ActivationFunctionType.Copy
TANH = mybir.ActivationFunctionType.Tanh
MULT = mybir.AluOpType.mult
ADD = mybir.AluOpType.add
SUBTRACT = mybir.AluOpType.subtract

P = 128
EDGE = 64
SHARE = 192
SHARE_PIECE = 64
LAST_GATHERS = (320, 256, 256)
PASS = 128
VECTOR_BANKS = (5, 6)
SCALAR_LOSERS = ((64, 128), (128, 256), (256, 384), (384, 512))
VECTOR_LOSERS = (0, 64)
COMPARES = ((128, 128), (64, 64), (64, 64))


def tile_picked_ranknet_tanh_e_kernel(tc, xT, w1, offs, win, lose, out):
    nc = tc.nc
    own = S - SHARE
    with ExitStack() as ctx:
        keep = ctx.enter_context(tc.tile_pool(name="keep", bufs=1))
        psum = ctx.enter_context(tc.psum_pool(name="psum", bufs=1))

        offs_t = keep.tile([P, S // 16], U16, name="offs_t")
        win_t = keep.tile([P, V // 16], U16, name="win_t")
        lose_t = keep.tile([P, V // 16], U16, name="lose_t")
        w_raw = keep.tile([P, 4, N], F32, name="w_raw")
        x_rows = xT.rearrange("(p j) t -> p j t", j=4)

        raw = [keep.tile([P, T], F32, name="raw_%d" % j) for j in range(4)]
        nc.sync.dma_start(out=raw[0][:], in_=x_rows[:, 0, :])
        nc.sync.dma_start(offs_t[:], offs)
        zeros = keep.tile([16, 16], F32, name="zeros")
        nc.vector.memset(zeros[:], 0.0)
        nc.scalar.dma_start(out=out[16:32, :16], in_=zeros[:])
        nc.scalar.dma_start(out=raw[1][:, T - EDGE :], in_=x_rows[:, 1, T - EDGE :])
        nc.sync.dma_start(out=raw[1][:, : T - EDGE], in_=x_rows[:, 1, : T - EDGE])
        for j in (2, 3):
            nc.sync.dma_start(out=raw[j][:], in_=x_rows[:, j, :])
        nc.sync.dma_start(out=w_raw[:], in_=w1.rearrange("(p j) n -> p j n", j=4))
        nc.sync.dma_start(lose_t[:], lose)
        nc.sync.dma_start(win_t[:], win)

        pairs = keep.tile([P, 2, 2 * own], BF16, name="pairs", tag="pairs_then_y", align_bytes=64)
        planes = keep.tile([P, 4, SHARE], BF16, name="planes", align_bytes=64)
        woven = keep.tile([P, 4 * S], BF16, name="woven", align_bytes=64)
        pair_words = pairs[:].bitcast(U32)

        def gather(j, s0, s1):
            slot = pairs[:, j // 2, 2 * (s0 - SHARE) : 2 * (s1 - SHARE)].rearrange("p (s e) -> p s e", e=2)[:, :, j % 2]
            nc.vector.tensor_copy(out=slot, in_=raw[j][:].indirect(offs_t[:, s0 // 16 : s1 // 16]))

        def gather_share(j, s0, s1):
            nc.scalar.activation(out=planes[:, j, s0:s1], in_=raw[j][:].indirect(offs_t[:, s0 // 16 : s1 // 16]), func=COPY)

        def lay_share(u, s0, s1):
            nc.scalar.copy(
                out=woven[:, 4 * s0 : 4 * s1].rearrange("p (s u e) -> p s u e", u=2, e=2)[:, :, u, :],
                in_=planes[:, 2 * u : 2 * u + 2, s0:s1].rearrange("p e s -> p s e"),
            )

        def weave(s0, s1):
            nc.scalar.copy(
                out=woven[:, 4 * s0 : 4 * s1].bitcast(U32).rearrange("p (s u) -> p s u", u=2),
                in_=pair_words[:, :, s0 - SHARE : s1 - SHARE].rearrange("p u s -> p s u"),
            )

        for j in range(3):
            gather(j, SHARE, S)
            gather_share(j, 0, SHARE)
            if j == 1:
                lay_share(0, 0, SHARE)

        w_bf = keep.tile([P, N * 4], BF16, name="w_bf", align_bytes=64)
        w_codes = keep.tile([P, N], U32, name="w_codes", align_bytes=64)
        w_scales = keep.tile([P, N], U8, name="w_scales", align_bytes=64)

        for s0 in range(0, SHARE, SHARE_PIECE):
            gather_share(3, s0, s0 + SHARE_PIECE)
        nc.gpsimd.tensor_scalar(
            out=woven[:, : 4 * SHARE_PIECE].rearrange("p (s u e) -> p s u e", u=2, e=2)[:, :, 1, :],
            in0=planes[:, 2:4, :SHARE_PIECE].rearrange("p e s -> p s e"),
            scalar1=1.0, scalar2=0.0, op0=MULT, op1=ADD,
        )
        nc.sync.dma_start(out=out[:16, :16], in_=raw[3][:16, :16])
        nc.gpsimd.tensor_scalar(
            out=w_bf[:].rearrange("p (n j) -> p n j", j=4), in0=w_raw[:].rearrange("p j n -> p n j"),
            scalar1=1.0, scalar2=0.0, op0=MULT, op1=ADD,
        )
        for s0 in range(SHARE_PIECE, SHARE, SHARE_PIECE):
            lay_share(1, s0, s0 + SHARE_PIECE)
        s0 = SHARE
        for width in LAST_GATHERS:
            gather(3, s0, s0 + width)
            if s0 + width < S:
                weave(s0, s0 + width)
            else:
                weave(s0, S - PASS)
                weave(S - PASS, S)
            s0 += width

        nc.vector.quantize_mx(out=w_codes[:].bitcast(FP8X4), scales=w_scales[:], in_=w_bf[:])
        y = keep.tile([P, S], F32, name="y", tag="pairs_then_y", align_bytes=64)
        starts = list(range(0, S, PASS))
        banks = []
        for s0 in starts:
            codes = keep.tile([P, PASS], U32, name="codes_%d" % s0, align_bytes=64)
            scales = keep.tile([P, PASS], U8, name="scales_%d" % s0, align_bytes=64)
            nc.vector.quantize_mx(out=codes[:].bitcast(FP8X4), scales=scales[:], in_=woven[:, 4 * s0 : 4 * (s0 + PASS)])
            acc = psum.tile([P, PASS], F32, name="acc_%d" % s0)
            nc.tensor.matmul_mx(
                out=acc[:],
                lhsT=w_codes[:].bitcast(FP8X4),
                lhsT_scale=w_scales[:],
                rhs=codes[:].bitcast(FP8X4),
                rhs_scale=scales[:],
                start=True,
                stop=True,
            )
            banks.append(acc)
        for i, acc in enumerate(banks):
            (nc.vector.tensor_copy if i in VECTOR_BANKS else nc.scalar.copy)(
                out=y[:, starts[i] : starts[i] + PASS], in_=acc[:]
            )

        y_lose = keep.tile([P, V], F32, name="y_lose")
        v0, v1 = VECTOR_LOSERS
        nc.vector.tensor_copy(out=y_lose[:, v0:v1], in_=y[:].indirect(lose_t[:, v0 // 16 : v1 // 16]))
        early0, early1 = SCALAR_LOSERS[-1]
        y_win = keep.tile([P, early1 - early0], F32, name="y_win")
        nc.vector.tensor_copy(out=y_win[:], in_=y[:].indirect(win_t[:, early0 // 16 : early1 // 16]))
        for v0, v1 in SCALAR_LOSERS:
            nc.scalar.activation(out=y_lose[:, v0:v1], in_=y[:].indirect(lose_t[:, v0 // 16 : v1 // 16]), func=COPY)
        v0 = 0
        for pieces in COMPARES:
            first = v0
            diff = keep.tile([P, sum(pieces)], F32, name="diff_%d" % first)
            res = keep.tile([P, sum(pieces)], F32, name="res_%d" % first)
            for width in pieces:
                nc.vector.tensor_tensor(
                    out=diff[:, v0 - first : v0 - first + width],
                    in0=y_win[:, v0 - early0 : v0 - early0 + width] if v0 >= early0 else y[:].indirect(win_t[:, v0 // 16 : (v0 + width) // 16]),
                    in1=y_lose[:, v0 : v0 + width],
                    op=SUBTRACT,
                )
                v0 += width
                piece = slice(v0 - first - width, v0 - first)
                nc.scalar.activation(out=res[:, piece], in_=diff[:, piece], func=TANH)
            queue = nc.scalar if v0 == V else nc.sync
            queue.dma_start(out=out[:, first:v0], in_=res[:])
